import numpy as np
import ml_dtypes


def mxq(x, axis, fmt="e4m3"):
    dtype, down = {"e4m3": (ml_dtypes.float8_e4m3fn, 7), "e5m2": (ml_dtypes.float8_e5m2, 14)}[fmt]
    v = np.moveaxis(np.asarray(x, np.float32).astype(ml_dtypes.bfloat16).astype(np.float64), axis, -1)
    blocks = v.reshape(v.shape[:-1] + (-1, 32))
    amax = np.abs(blocks).max(-1, keepdims=True)
    byte = np.maximum(np.where(amax > 0, np.frexp(amax)[1] - 1 + 127, 0) - down, 1)
    scale = np.exp2(byte - 127.0)
    codes = (blocks / scale).astype(np.float32).astype(dtype).astype(np.float64)
    return np.moveaxis((codes * scale).reshape(v.shape), -1, axis)


WIDE = False


def mx_kscale(k):
    if not WIDE:
        return np.ones(k)
    levels = np.array([10, -10, 5, -5, 0])
    if k % 512:
        return np.exp2(np.random.permutation(np.resize(levels, k // 32))).repeat(32)
    a = np.empty((k // 512, 16))
    for p in range(k // 512):
        a[p, :8] = np.random.permutation(np.resize(levels, 8))
        for g in range(8):
            far = levels[np.abs(levels - a[p, g]) >= 10]
            a[p, g + 8] = far[np.random.randint(len(far))]
    return np.exp2(a.ravel()).repeat(32)


def f64(x):
    return np.asarray(x).astype(np.float64)


def striped(idx):
    return np.tile(idx.reshape(-1, 16).T, (8, 1)).astype(np.uint16)


def unstriped(offs):
    return offs[:16].T.reshape(-1).astype(np.int64)


E2M1 = np.array([0.0, 0.5, 1.0, 1.5, 2.0, 3.0, 4.0, 6.0, -0.0, -0.5, -1.0, -1.5, -2.0, -3.0, -4.0, -6.0])


def pack_weight(w, fmt):
    k, n = w.shape
    w = f64(np.asarray(w, np.float32).astype(ml_dtypes.bfloat16)).reshape(k // 32, 32, n)
    amax = np.abs(w).max(1)
    if fmt == "e4m3":
        byte = np.frexp(amax)[1] - 1 + 127 - 7
    else:
        mant, ex = np.frexp(amax / 6.0)
        byte = np.where(mant > 0.5, ex, ex - 1) + 127
    byte = np.clip(np.where(amax > 0, byte, 1), 1, 254)
    scaled = (w * np.exp2(127.0 - byte)[:, None, :]).reshape(k, n).astype(np.float32)
    by_word = np.ascontiguousarray(scaled.reshape(k // 512, 128, 4, n).transpose(0, 1, 3, 2))
    if fmt == "e4m3":
        words = by_word.astype(ml_dtypes.float8_e4m3fn).view(np.uint8)
    else:
        c = by_word.astype(ml_dtypes.float4_e2m1fn).view(np.uint8) & 0xF
        words = (c[..., 0::2] | (c[..., 1::2] << 4)).reshape(k // 512, 128, 2 * n)
    return np.ascontiguousarray(words), np.ascontiguousarray(byte.astype(np.uint8).reshape(k // 512, 16, n))


def unpack_weight(words, scales, fmt):
    g, _, n = scales.shape
    words = np.ascontiguousarray(words).reshape(g, 128, n, -1)
    if fmt == "e4m3":
        vals = words.view(ml_dtypes.float8_e4m3fn).astype(np.float64)
    else:
        nib = np.empty((g, 128, n, 4), np.uint8)
        nib[..., 0::2] = words & 0xF
        nib[..., 1::2] = words >> 4
        vals = E2M1[nib]
    vals = vals * np.repeat(np.exp2(scales.astype(np.float64) - 127.0), 8, axis=1)[..., None]
    return vals.transpose(0, 1, 3, 2).reshape(g * 512, n)


def gelu(v):
    return 0.5 * v * (1.0 + np.tanh(np.sqrt(2.0 / np.pi) * (v + 0.044715 * v**3)))


K, K2, T, S, H, N, T2 = 1024, 512, 2048, 512, 1024, 384, 1024

def setup_inputs():
    n = np.random.standard_normal
    s, s2, u = mx_kscale(K)[:, None], mx_kscale(K2)[:, None], mx_kscale(H)[:, None]
    tab_words, tab_scales = pack_weight(n((K, T)) * s, "e4m3")
    tab2_words, tab2_scales = pack_weight(n((K2, T)) * s2, "e4m3")
    w2_words, w2_scales = pack_weight(n((K2, H)) / np.sqrt(K2) / s2 * u.T, "e2m1")
    w4_words, w4_scales = pack_weight(n((H, N)) / np.sqrt(H) / u, "e4m3")
    return {
        "tab_words": tab_words, "tab_scales": tab_scales,
        "tab2_words": tab2_words, "tab2_scales": tab2_scales,
        "offs": striped(np.random.permutation(T)[:S]),
        "offs2": striped(np.random.permutation(T)[:S]),
        "offs3": striped(np.random.permutation(T2)[:S]),
        "offs4": striped(np.random.permutation(T2)[:S]),
        "w1": (1.5 * n((K, H)) / np.sqrt(K) / s).astype(np.float32),
        "gain1": (np.exp(0.3 * n(H)) * u[:, 0]).astype(np.float32),
        "w2_words": w2_words, "w2_scales": w2_scales,
        "low2": (0.5 * n(H) * u[:, 0]).astype(np.float32),
        "wg1": np.exp(0.3 * n((128, S))).astype(np.float32),
        "wg2": np.exp(0.3 * n((128, S))).astype(np.float32),
        "base": (0.7 * n((H, T2)) * u).astype(np.float32),
        "w3": (n((H, H)) / np.sqrt(H) / u * u.T).astype(np.float32),
        "w4_words": w4_words, "w4_scales": w4_scales,
    }

def reference(tab_words, tab_scales, tab2_words, tab2_scales, offs, offs2, offs3, offs4, w1, gain1, w2_words, w2_scales, low2, wg1, wg2, base, w3, w4_words, w4_scales):
    v = unpack_weight(tab_words, tab_scales, "e4m3")[:, unstriped(offs)]
    v2 = unpack_weight(tab2_words, tab2_scales, "e4m3")[:, unstriped(offs2)]
    h1 = f64(gain1)[:, None] * np.tanh(mxq(f64(w1), 0, "e4m3").T @ v)
    h2 = np.maximum(unpack_weight(w2_words, w2_scales, "e2m1").T @ v2, f64(low2)[:, None])
    pa = np.zeros((H, T2))
    pa[:, unstriped(offs3)] = np.tile(f64(wg1), (H // 128, 1)) * h1
    pb = np.zeros((H, T2))
    pb[:, unstriped(offs4)] = np.tile(f64(wg2), (H // 128, 1)) * h2
    z = pa + pb + f64(base)
    y = np.maximum(mxq(f64(w3), 0, "e4m3").T @ mxq(z, 0, "e4m3"), z)
    return unpack_weight(w4_words, w4_scales, "e4m3").T @ mxq(y, 0, "e4m3")

@@ -1,0 +1,386 @@
+from contextlib import ExitStack
+
+import concourse.mybir as mybir
+from concourse.masks import make_identity
+
+K, K2, T, S, H, N, T2 = 1024, 512, 2048, 512, 1024, 384, 1024
+FLOPS = 2 * (K * H * S + K2 * H * S + H * H * T2 + H * N * T2)
+
+F32 = mybir.dt.float32
+BF16 = mybir.dt.bfloat16
+I32 = mybir.dt.int32
+U32 = mybir.dt.uint32
+U16 = mybir.dt.uint16
+U8 = mybir.dt.uint8
+FP8X4 = mybir.dt.float8_e4m3fn_x4
+FP4X4 = mybir.dt.float4_e2m1fn_x4
+ALU = mybir.AluOpType
+ACT = mybir.ActivationFunctionType
+
+P = 128
+PACK = 4
+KP = P * PACK
+SLICES = H // P
+JT = T2 // P
+W1_CHUNK = 256
+LEAD = 3
+
+
+def tile_list_elastography_line_scores_kernel(
+    tc, tab_words, tab_scales, tab2_words, tab2_scales, offs, offs2, offs3, offs4,
+    w1, gain1, w2_words, w2_scales, low2, wg1, wg2, base, w3, w4_words, w4_scales, out,
+):
+    nc = tc.nc
+    with ExitStack() as ctx:
+        lists = ctx.enter_context(tc.tile_pool(name="lists", bufs=1))
+        keep = ctx.enter_context(tc.tile_pool(name="keep", bufs=1))
+        ring = ctx.enter_context(tc.tile_pool(name="ring", bufs=1))
+        psum = ctx.enter_context(tc.psum_pool(name="psum", bufs=1))
+
+        def load_list(src, name):
+            t = lists.tile([P, S // 16], U16, name=name)
+            nc.sync.dma_start(t[:], src)
+            return t
+
+        def zeroed_plane(width, name):
+            t = keep.tile([P, width], U8, name=name, align_bytes=64)
+            nc.vector.memset(t[:].bitcast(I32), 0)
+            return t
+
+        def load_plane(t, scales):
+            passes = scales.shape[0]
+            for q in range(4):
+                nc.sync.dma_start(
+                    out=t[32 * q : 32 * q + 4 * passes, :].bitcast(I32),
+                    in_=scales[:, 4 * q : 4 * q + 4, :].bitcast(I32),
+                )
+
+        def load_words(words, name):
+            t = keep.tile([P, words.shape[1]], I32, name=name, align_bytes=64)
+            nc.sync.dma_start(out=t[:], in_=words.rearrange("p t i -> p (t i)").bitcast(I32))
+            return t
+
+        def gather(window, dtype, idx, name):
+            g = keep.tile([P, S], dtype, name=name, align_bytes=64)
+            nc.vector.tensor_copy(g[:], window.indirect(idx[:]))
+            return g
+
+        t2s = zeroed_plane(T, "t2s")
+        w2s = zeroed_plane(H, "w2s")
+        vec = keep.tile([P, P], F32, name="vec")
+        nc.gpsimd.memset(vec[:], 0.0)
+        nc.gpsimd.dma_start(out=vec[0:SLICES, :], in_=low2.rearrange("(s p) -> s p", p=P))
+        nc.gpsimd.dma_start(out=vec[SLICES : 2 * SLICES, :], in_=gain1.rearrange("(s p) -> s p", p=P))
+        ident = keep.tile([P, P], F32, name="ident")
+        make_identity(nc, ident[:])
+
+        t1s = zeroed_plane(T, "t1s")
+        t2w = load_words(tab2_words[0], "t2w")
+        load_plane(t2s, tab2_scales)
+        idx2 = load_list(offs2, "idx2")
+        w2w = keep.tile([P, 2 * H], U8, name="w2w", align_bytes=64)
+        nc.sync.dma_start(out=w2w[:].bitcast(I32), in_=w2_words[0].bitcast(I32))
+        load_plane(w2s, w2_scales)
+        idx4 = load_list(offs4, "idx4")
+        wg2t = keep.tile([P, S], F32, name="wg2t")
+        nc.sync.dma_start(out=wg2t[:], in_=wg2)
+        t1w = [load_words(tab_words[0], "t1w0")]
+        idx1 = load_list(offs, "idx1")
+        t1w.append(load_words(tab_words[1], "t1w1"))
+        load_plane(t1s, tab_scales)
+
+        pb = []
+        for i in range(LEAD + 1):
+            page = keep.tile([P, T2], F32, name="pb%d" % i)
+            nc.vector.memset(page[:], 0.0)
+            pb.append(page)
+        pa = []
+        for i in range(2):
+            page = keep.tile([P, T2], F32, name="pa%d" % i)
+            nc.gpsimd.memset(page[:], 0.0)
+            pa.append(page)
+        w4s = keep.tile([P, N], U8, name="w4s", align_bytes=64)
+        nc.gpsimd.memset(w4s[:].bitcast(I32), 0)
+
+        vec_ps = psum.tile([P, KP], F32, name="vec_ps", tag="hb", bufs=2)
+        nc.tensor.transpose(vec_ps[:, 0:P], vec[:], ident[:])
+        cols = keep.tile([P, 2 * SLICES], F32, name="cols")
+        nc.scalar.copy(cols[:], vec_ps[:, 0 : 2 * SLICES])
+
+        v2s = gather(t2s[:], U8, idx2, "v2s")
+        v2w = gather(t2w[:].bitcast(U32), U32, idx2, "v2w")
+
+        w1c = keep.tile([P, 2, H], U32, name="w1c", align_bytes=64)
+        w1s = keep.tile([P, 2, H], U8, name="w1s", align_bytes=64)
+
+        def w1_chunk(c):
+            cs = slice(c * W1_CHUNK, (c + 1) * W1_CHUNK)
+            for a in range(2):
+                raw = ring.tile([P, PACK, W1_CHUNK], F32, name="raw1", tag="raw", bufs=3)
+                nc.sync.dma_start(
+                    out=raw[:], in_=w1[a * KP : (a + 1) * KP, cs].rearrange("(p j) c -> p j c", j=PACK)
+                )
+                if c == 0 and a == 1:
+                    grp = ring.tile([P, W1_CHUNK * PACK], BF16, name="grp1", tag="hold", bufs=1, align_bytes=64)
+                else:
+                    grp = ring.tile([P, W1_CHUNK * PACK], BF16, name="grp1", tag="grp1", bufs=2, align_bytes=64)
+                nc.scalar.copy(
+                    grp[:].rearrange("p (c i j) -> p c j i", i=4, j=PACK),
+                    raw[:].rearrange("p j (c i) -> p c j i", i=4),
+                )
+                nc.vector.quantize_mx(out=w1c[:, a, cs].bitcast(FP8X4), scales=w1s[:, a, cs], in_=grp[:])
+
+        w3g = {}
+
+        def w3_cast(a, b):
+            raw = ring.tile([P, PACK, KP], F32, name="raw3", tag="raw", bufs=3)
+            nc.sync.dma_start(
+                out=raw[:],
+                in_=w3[a * KP : (a + 1) * KP, b * KP : (b + 1) * KP].rearrange("(p j) c -> p j c", j=PACK),
+            )
+            grp = keep.tile([P, KP * PACK], BF16, name="w3g%d%d" % (a, b), align_bytes=64)
+            nc.scalar.copy(
+                grp[:].rearrange("p (t q j) -> p q j t", t=PACK, j=PACK),
+                raw[:].rearrange("p j (q t) -> p q j t", t=PACK),
+            )
+            w3g[(a, b)] = grp
+
+        h1 = {}
+        h2 = {}
+        base_t = {}
+        fw = {}
+        zt = {}
+        zf = {}
+        zb0 = keep.tile([P, JT, KP], BF16, name="zb0", align_bytes=64)
+
+        def make_h2(s):
+            acc = psum.tile([P, S], F32, name="h2_ps", tag="hb", bufs=2)
+            nc.tensor.matmul_mx(
+                out=acc[:], lhsT=w2w[:, 2 * P * s : 2 * P * (s + 1)].bitcast(FP4X4),
+                lhsT_scale=w2s[:, P * s : P * (s + 1)], rhs=v2w[:].bitcast(FP8X4), rhs_scale=v2s[:],
+                start=True, stop=True,
+            )
+            h = ring.tile([P, S], F32, name="h2", tag="h", bufs=4)
+            if s == 0:
+                nc.vector.tensor_scalar(h[:], acc[:], cols[:, 0:1], None, ALU.max)
+            else:
+                nc.scalar.copy(h[:], acc[:])
+            h2[s] = h
+
+        def clamp_h2(s):
+            src = h2[s]
+            if s == LEAD - 1:
+                h2[s] = ring.tile([P, S], F32, name="h2_held", tag="hold", bufs=1, align_bytes=64)
+            nc.vector.tensor_scalar(h2[s][:], src[:], cols[:, s : s + 1], None, ALU.max)
+
+        def make_h1(s):
+            acc = psum.tile([P, S], F32, name="h1_ps", tag="hb", bufs=2)
+            for a in range(2):
+                nc.tensor.matmul_mx(
+                    out=acc[:], lhsT=w1c[:, a, P * s : P * (s + 1)].bitcast(FP8X4),
+                    lhsT_scale=w1s[:, a, P * s : P * (s + 1)], rhs=v1w[a][:].bitcast(FP8X4),
+                    rhs_scale=v1s[4 * a : P, :], start=(a == 0), stop=(a == 1),
+                )
+            h = ring.tile([P, S], F32, name="h1", tag="h", bufs=4)
+            nc.scalar.activation(h[:], acc[:], ACT.Tanh)
+            nc.scalar.activation(h[:], h[:], ACT.Copy, scale=cols[:, SLICES + s : SLICES + s + 1])
+            h1[s] = h
+
+        def load_base(s):
+            t = ring.tile([P, T2], F32, name="base_t", tag="base", bufs=4)
+            nc.sync.dma_start(out=t[:], in_=base[s * P : (s + 1) * P, :])
+            base_t[s] = t
+
+        def add_turned(s, src, first, last):
+            for half in range(2):
+                if first:
+                    fw[(s, half)] = psum.tile([P, 4, P], F32, name="fw", tag="fw", bufs=4)
+                for g in range(4):
+                    jt = 4 * half + g
+                    nc.tensor.matmul(
+                        fw[(s, half)][:, g, :], src[:, jt * P : (jt + 1) * P], ident[:],
+                        start=(first and g == 0), stop=(last and g == 3), is_transpose=True,
+                    )
+                if last:
+                    a, quarter = divmod(s, 4)
+                    if quarter == 0:
+                        zt[(a, half)] = ring.tile([P, 4, PACK, P], F32, name="zt", tag="zt", bufs=4)
+                    nc.scalar.copy(
+                        zt[(a, half)][:, :, :, 32 * quarter : 32 * (quarter + 1)],
+                        fw[(s, half)][:].rearrange("j g (q t) -> j g t q", t=PACK),
+                    )
+
+        def turn_back(a, jt, zb):
+            bank = psum.tile([P, PACK, P], F32, name="bk", tag="bk", bufs=2)
+            for t in range(PACK):
+                nc.tensor.transpose(bank[:, t, :], zt[(a, jt // 4)][:, jt % 4, t, :], ident[:])
+            if jt % 2 == 0:
+                if a == 0:
+                    zf[(a, jt // 2)] = keep.tile([P, 2, KP], F32, name="zf0%d" % (jt // 2))
+                else:
+                    zf[(a, jt // 2)] = ring.tile([P, 2, KP], F32, name="zf1", tag="base", bufs=4)
+            woven = bank[:].rearrange("p t j -> p j t")
+            nc.scalar.copy(zb.rearrange("p (j t) -> p j t", t=PACK), woven)
+            nc.scalar.copy(zf[(a, jt // 2)][:, jt % 2, :].rearrange("p (j t) -> p j t", t=PACK), woven)
+
+        def scatter(page, idx, h, wg):
+            nc.vector.tensor_tensor(page[:].indirect(idx[:]), h[:], wg[:], ALU.mult)
+
+        steps = [("b", s) for s in range(LEAD)]
+        for s in range(SLICES):
+            steps.append(("a", s))
+            if s + LEAD < SLICES:
+                steps.append(("b", s + LEAD))
+
+        def make_h(k):
+            kind, s = steps[k]
+            if kind == "a":
+                make_h1(s)
+            else:
+                make_h2(s)
+
+        make_h(0)
+        make_h(1)
+        w1_chunk(0)
+        idx3 = load_list(offs3, "idx3")
+        wg1t = ring.tile([P, S], F32, name="wg1t", tag="late", bufs=1, align_bytes=64)
+        nc.sync.dma_start(out=wg1t[:], in_=wg1)
+        for k in range(len(steps)):
+            kind, s = steps[k]
+            if k == 1:
+                v1w = [gather(t1w[a][:].bitcast(U32), U32, idx1, "v1w%d" % a) for a in range(2)]
+                v1s = gather(t1s[:], U8, idx1, "v1s")
+            if k + 2 < len(steps):
+                make_h(k + 2)
+            if k >= 1 and steps[k - 1][0] == "a":
+                add_turned(steps[k - 1][1], pa[steps[k - 1][1] % 2], False, True)
+            if k in (1, 3, 5):
+                w1_chunk(k // 2 + 1)
+            if k in (2, 4, 6, 7):
+                i = (2, 4, 6, 7).index(k)
+                w3_cast(i // 2, i % 2)
+            if k == 1:
+                load_base(0)
+            if kind == "a":
+                if s + 1 < SLICES:
+                    load_base(s + 1)
+                add_turned(s, base_t[s], True, False)
+                add_turned(s, pb[s % (LEAD + 1)], False, False)
+            if k == 8:
+                load_plane(w4s, w4_scales)
+                w4w = [load_words(w4_words[a], "w4w%d" % a) for a in range(2)]
+            if 10 <= k < 14:
+                for jt in (2 * (k - 10), 2 * (k - 10) + 1):
+                    turn_back(0, jt, zb0[:, jt, :])
+            if k + 1 < len(steps) and steps[k + 1][0] == "b":
+                clamp_h2(steps[k + 1][1])
+            if kind == "a":
+                scatter(pa[s % 2], idx3, h1[s], wg1t)
+            else:
+                scatter(pb[s % (LEAD + 1)], idx4, h2[s], wg2t)
+        add_turned(SLICES - 1, pa[(SLICES - 1) % 2], False, True)
+
+        late = ring.tile([P, 3 * H], U32, name="late", tag="late", bufs=1, align_bytes=64)
+        late_s = keep.tile([P, 3 * H], U8, name="late_s", align_bytes=64)
+
+        def w3_cols(a, b, t):
+            c0 = a * H + b * KP + t * P
+            return slice(c0, c0 + P)
+
+        def quant_late(c0, src):
+            w = src.shape[1] // PACK
+            nc.vector.quantize_mx(out=late[:, c0 : c0 + w].bitcast(FP8X4), scales=late_s[:, c0 : c0 + w], in_=src)
+
+        zb0_flat = zb0[:].rearrange("p j c -> p (j c)")
+        quant_late(2 * H, zb0_flat[:, 0 : 4 * KP])
+        for b in range(2):
+            quant_late(b * KP, w3g[(0, b)][:])
+        for b in range(2):
+            quant_late(H + b * KP, w3g[(1, b)][:])
+        quant_late(2 * H + KP, zb0_flat[:, 4 * KP : 8 * KP])
+
+        acc3 = {}
+        z1 = {}
+        yq = {}
+
+        def product_pass(jt, b, a):
+            if a == 0:
+                acc3[(jt, b)] = psum.tile([P, PACK, P], F32, name="acc3", tag="fw", bufs=4)
+                rhs = late[:, 2 * H + jt * P : 2 * H + (jt + 1) * P]
+                rhs_scale = late_s[:, 2 * H + jt * P : 2 * H + (jt + 1) * P]
+            else:
+                rhs, rhs_scale = z1[jt][0][:], z1[jt][1][:]
+            for t in range(PACK):
+                cs = w3_cols(a, b, t)
+                nc.tensor.matmul_mx(
+                    out=acc3[(jt, b)][:, t, :], lhsT=late[:, cs].bitcast(FP8X4), lhsT_scale=late_s[:, cs],
+                    rhs=rhs.bitcast(FP8X4), rhs_scale=rhs_scale,
+                    start=(a == 0 and t == 0), stop=(a == 1 and t == PACK - 1),
+                )
+
+        def make_z1(jt):
+            zb = ring.tile([P, KP], BF16, name="zb1", tag="zb1", bufs=3, align_bytes=64)
+            turn_back(1, jt, zb[:])
+            codes = ring.tile([P, P], U32, name="z1c", tag="z1c", bufs=3, align_bytes=64)
+            scales = ring.tile([P, P], U8, name="z1s", tag="z1s", bufs=3, align_bytes=64)
+            nc.vector.quantize_mx(out=codes[:].bitcast(FP8X4), scales=scales[:], in_=zb[:])
+            z1[jt] = (codes, scales)
+
+        yb = {}
+
+        def make_y(jt, b):
+            if b == 0:
+                yb[jt] = ring.tile([P, 2, KP], BF16, name="yb", tag="yb", bufs=2, align_bytes=64)
+            nc.vector.tensor_tensor(
+                yb[jt][:, b, :].rearrange("p (j t) -> p j t", t=PACK),
+                acc3[(jt, b)][:].rearrange("p t j -> p j t"),
+                zf[(b, jt // 2)][:, jt % 2, :].rearrange("p (j t) -> p j t", t=PACK),
+                ALU.max,
+            )
+
+        def quant_y(jt):
+            codes = ring.tile([P, 2 * P], U32, name="yc", tag="yc", bufs=2, align_bytes=64)
+            scales = ring.tile([P, 2 * P], U8, name="ys", tag="ys", bufs=2, align_bytes=64)
+            nc.vector.quantize_mx(
+                out=codes[:].bitcast(FP8X4), scales=scales[:], in_=yb[jt][:].rearrange("p b c -> p (b c)")
+            )
+            yq[jt] = (codes, scales)
+
+        def scores(jt):
+            codes, scales = yq[jt]
+            acc = psum.tile([P, N // P, P], F32, name="o_ps", tag="hb", bufs=2)
+            for n in range(N // P):
+                for b in range(2):
+                    nc.tensor.matmul_mx(
+                        out=acc[:, n, :], lhsT=w4w[b][:, n * P : (n + 1) * P].bitcast(FP8X4),
+                        lhsT_scale=w4s[4 * b : P, n * P : (n + 1) * P],
+                        rhs=codes[:, b * P : (b + 1) * P].bitcast(FP8X4), rhs_scale=scales[:, b * P : (b + 1) * P],
+                        start=(b == 0), stop=(b == 1),
+                    )
+            res = ring.tile([P, N // P, P], F32, name="res", tag="res", bufs=3)
+            nc.scalar.copy(res[:], acc[:])
+            nc.sync.dma_start(
+                out=out[:, jt * P : (jt + 1) * P].rearrange("(n p) j -> p n j", p=P), in_=res[:]
+            )
+
+        for jt in range(2):
+            for b in range(2):
+                product_pass(jt, b, 0)
+        make_z1(0)
+        make_z1(1)
+        for jt in range(JT):
+            for b in range(2):
+                product_pass(jt, b, 1)
+            if jt + 2 < JT:
+                make_z1(jt + 2)
+            make_y(jt, 0)
+            if jt >= 1:
+                quant_y(jt - 1)
+            make_y(jt, 1)
+            if jt + 2 < JT:
+                for b in range(2):
+                    product_pass(jt + 2, b, 0)
+            if jt >= 1:
+                scores(jt - 1)
+        quant_y(JT - 1)
+        scores(JT - 1)

@@ -24,6 +24,8 @@ SLICES = H // P
 JT = T2 // P
 W1_CHUNK = 256
 LEAD = 3
+BANK_BYTES = 2048
+EARLY = 2
 
 
 def tile_list_elastography_line_scores_kernel(
@@ -36,6 +38,9 @@ def tile_list_elastography_line_scores_kernel(
         keep = ctx.enter_context(tc.tile_pool(name="keep", bufs=1))
         ring = ctx.enter_context(tc.tile_pool(name="ring", bufs=1))
         psum = ctx.enter_context(tc.psum_pool(name="psum", bufs=1))
+
+        def bank(first, count, shape, name):
+            return psum.tile(shape, F32, name=name, tag="bank%d_%d" % (first, count), bufs=1, offset=first * BANK_BYTES)
 
         def load_list(src, name):
             t = lists.tile([P, S // 16], U16, name=name)
@@ -92,17 +97,17 @@ def tile_list_elastography_line_scores_kernel(
         pb = []
         for i in range(LEAD + 1):
             page = keep.tile([P, T2], F32, name="pb%d" % i)
-            nc.vector.memset(page[:], 0.0)
+            nc.vector.memset(page[:].bitcast(I32), 0)
             pb.append(page)
         pa = []
         for i in range(2):
             page = keep.tile([P, T2], F32, name="pa%d" % i)
-            nc.gpsimd.memset(page[:], 0.0)
+            nc.vector.memset(page[:].bitcast(I32), 0)
             pa.append(page)
         w4s = keep.tile([P, N], U8, name="w4s", align_bytes=64)
         nc.gpsimd.memset(w4s[:].bitcast(I32), 0)
 
-        vec_ps = psum.tile([P, KP], F32, name="vec_ps", tag="hb", bufs=2)
+        vec_ps = bank(7, 1, [P, KP], "vec_ps")
         nc.tensor.transpose(vec_ps[:, 0:P], vec[:], ident[:])
         cols = keep.tile([P, 2 * SLICES], F32, name="cols")
         nc.scalar.copy(cols[:], vec_ps[:, 0 : 2 * SLICES])
@@ -110,40 +115,46 @@ def tile_list_elastography_line_scores_kernel(
         v2s = gather(t2s[:], U8, idx2, "v2s")
         v2w = gather(t2w[:].bitcast(U32), U32, idx2, "v2w")
 
-        w1c = keep.tile([P, 2, H], U32, name="w1c", align_bytes=64)
-        w1s = keep.tile([P, 2, H], U8, name="w1s", align_bytes=64)
+        w1c = keep.tile([P, 2 * H], U32, name="w1c", align_bytes=64)
+        w1s = keep.tile([P, 2 * H], U8, name="w1s", align_bytes=64)
 
         def w1_chunk(c):
             cs = slice(c * W1_CHUNK, (c + 1) * W1_CHUNK)
+            tag = "hold" if c == 0 else "grp1"
+            grp = ring.tile([P, 2 * W1_CHUNK * PACK], BF16, name="grp1", tag=tag, bufs=1, align_bytes=64)
             for a in range(2):
-                raw = ring.tile([P, PACK, W1_CHUNK], F32, name="raw1", tag="raw", bufs=3)
+                raw = ring.tile([P, PACK, W1_CHUNK], F32, name="raw1", tag="raw", bufs=3, align_bytes=64)
                 nc.sync.dma_start(
                     out=raw[:], in_=w1[a * KP : (a + 1) * KP, cs].rearrange("(p j) c -> p j c", j=PACK)
                 )
-                if c == 0 and a == 1:
-                    grp = ring.tile([P, W1_CHUNK * PACK], BF16, name="grp1", tag="hold", bufs=1, align_bytes=64)
-                else:
-                    grp = ring.tile([P, W1_CHUNK * PACK], BF16, name="grp1", tag="grp1", bufs=2, align_bytes=64)
                 nc.scalar.copy(
-                    grp[:].rearrange("p (c i j) -> p c j i", i=4, j=PACK),
+                    grp[:, a * W1_CHUNK * PACK : (a + 1) * W1_CHUNK * PACK].rearrange(
+                        "p (c i j) -> p c j i", i=4, j=PACK
+                    ),
                     raw[:].rearrange("p j (c i) -> p c j i", i=4),
                 )
-                nc.vector.quantize_mx(out=w1c[:, a, cs].bitcast(FP8X4), scales=w1s[:, a, cs], in_=grp[:])
+            both = slice(2 * c * W1_CHUNK, 2 * (c + 1) * W1_CHUNK)
+            nc.vector.quantize_mx(out=w1c[:, both].bitcast(FP8X4), scales=w1s[:, both], in_=grp[:])
+
+        def w1_cols(a, s):
+            c, half = divmod(s, 2)
+            c0 = (2 * c + a) * W1_CHUNK + half * P
+            return slice(c0, c0 + P)
 
         w3g = {}
 
         def w3_cast(a, b):
-            raw = ring.tile([P, PACK, KP], F32, name="raw3", tag="raw", bufs=3)
+            raw = ring.tile([P, PACK, KP], F32, name="raw3", tag="raw", bufs=3, align_bytes=64)
             nc.sync.dma_start(
                 out=raw[:],
                 in_=w3[a * KP : (a + 1) * KP, b * KP : (b + 1) * KP].rearrange("(p j) c -> p j c", j=PACK),
             )
-            grp = keep.tile([P, KP * PACK], BF16, name="w3g%d%d" % (a, b), align_bytes=64)
+            if b == 0:
+                w3g[a] = keep.tile([P, 2 * KP * PACK], BF16, name="w3g%d" % a, align_bytes=64)
             nc.scalar.copy(
-                grp[:].rearrange("p (t q j) -> p q j t", t=PACK, j=PACK),
+                w3g[a][:, b * KP * PACK : (b + 1) * KP * PACK].rearrange("p (t q j) -> p q j t", t=PACK, j=PACK),
                 raw[:].rearrange("p j (q t) -> p q j t", t=PACK),
             )
-            w3g[(a, b)] = grp
 
         h1 = {}
         h2 = {}
@@ -151,10 +162,10 @@ def tile_list_elastography_line_scores_kernel(
         fw = {}
         zt = {}
         zf = {}
-        zb0 = keep.tile([P, JT, KP], BF16, name="zb0", align_bytes=64)
+        zb0 = keep.tile([P, JT * KP], BF16, name="zb0", align_bytes=64)
 
-        def make_h2(s):
-            acc = psum.tile([P, S], F32, name="h2_ps", tag="hb", bufs=2)
+        def make_h2(s, b):
+            acc = bank(b, 1, [P, S], "h2_ps")
             nc.tensor.matmul_mx(
                 out=acc[:], lhsT=w2w[:, 2 * P * s : 2 * P * (s + 1)].bitcast(FP4X4),
                 lhsT_scale=w2s[:, P * s : P * (s + 1)], rhs=v2w[:].bitcast(FP8X4), rhs_scale=v2s[:],
@@ -173,12 +184,12 @@ def tile_list_elastography_line_scores_kernel(
                 h2[s] = ring.tile([P, S], F32, name="h2_held", tag="hold", bufs=1, align_bytes=64)
             nc.vector.tensor_scalar(h2[s][:], src[:], cols[:, s : s + 1], None, ALU.max)
 
-        def make_h1(s):
-            acc = psum.tile([P, S], F32, name="h1_ps", tag="hb", bufs=2)
+        def make_h1(s, b):
+            acc = bank(b, 1, [P, S], "h1_ps")
             for a in range(2):
                 nc.tensor.matmul_mx(
-                    out=acc[:], lhsT=w1c[:, a, P * s : P * (s + 1)].bitcast(FP8X4),
-                    lhsT_scale=w1s[:, a, P * s : P * (s + 1)], rhs=v1w[a][:].bitcast(FP8X4),
+                    out=acc[:], lhsT=w1c[:, w1_cols(a, s)].bitcast(FP8X4),
+                    lhsT_scale=w1s[:, w1_cols(a, s)], rhs=v1w[a][:].bitcast(FP8X4),
                     rhs_scale=v1s[4 * a : P, :], start=(a == 0), stop=(a == 1),
                 )
             h = ring.tile([P, S], F32, name="h1", tag="h", bufs=4)
@@ -194,7 +205,7 @@ def tile_list_elastography_line_scores_kernel(
         def add_turned(s, src, first, last):
             for half in range(2):
                 if first:
-                    fw[(s, half)] = psum.tile([P, 4, P], F32, name="fw", tag="fw", bufs=4)
+                    fw[(s, half)] = bank(2 + 2 * (s % 2) + half, 1, [P, 4, P], "fw")
                 for g in range(4):
                     jt = 4 * half + g
                     nc.tensor.matmul(
@@ -204,24 +215,27 @@ def tile_list_elastography_line_scores_kernel(
                 if last:
                     a, quarter = divmod(s, 4)
                     if quarter == 0:
-                        zt[(a, half)] = ring.tile([P, 4, PACK, P], F32, name="zt", tag="zt", bufs=4)
+                        zt[(a, half)] = ring.tile([P, 4, PACK, P], F32, name="zt", tag="zt", bufs=3)
                     nc.scalar.copy(
                         zt[(a, half)][:, :, :, 32 * quarter : 32 * (quarter + 1)],
                         fw[(s, half)][:].rearrange("j g (q t) -> j g t q", t=PACK),
                     )
 
-        def turn_back(a, jt, zb):
-            bank = psum.tile([P, PACK, P], F32, name="bk", tag="bk", bufs=2)
-            for t in range(PACK):
-                nc.tensor.transpose(bank[:, t, :], zt[(a, jt // 4)][:, jt % 4, t, :], ident[:])
-            if jt % 2 == 0:
-                if a == 0:
-                    zf[(a, jt // 2)] = keep.tile([P, 2, KP], F32, name="zf0%d" % (jt // 2))
-                else:
-                    zf[(a, jt // 2)] = ring.tile([P, 2, KP], F32, name="zf1", tag="base", bufs=4)
-            woven = bank[:].rearrange("p t j -> p j t")
-            nc.scalar.copy(zb.rearrange("p (j t) -> p j t", t=PACK), woven)
-            nc.scalar.copy(zf[(a, jt // 2)][:, jt % 2, :].rearrange("p (j t) -> p j t", t=PACK), woven)
+        def turn_back(a, pair, zb, first_bank):
+            banks = bank(first_bank, 2, [P, 2, PACK, P], "bk")
+            if a == 0:
+                zf[(a, pair)] = keep.tile([P, 2, KP], F32, name="zf0%d" % pair)
+            else:
+                zf[(a, pair)] = ring.tile([P, 2, KP], F32, name="zf1", tag="base", bufs=4)
+            for u in range(2):
+                jt = 2 * pair + u
+                for t in range(PACK):
+                    nc.tensor.transpose(banks[:, u, t, :], zt[(a, jt // 4)][:, jt % 4, t, :], ident[:])
+            for u in range(2):
+                jt = 2 * pair + u
+                woven = banks[:, u, :, :].rearrange("p t j -> p j t")
+                nc.scalar.copy(zb[:, jt * KP : (jt + 1) * KP].rearrange("p (j t) -> p j t", t=PACK), woven)
+                nc.scalar.copy(zf[(a, pair)][:, u, :].rearrange("p (j t) -> p j t", t=PACK), woven)
 
         def scatter(page, idx, h, wg):
             nc.vector.tensor_tensor(page[:].indirect(idx[:]), h[:], wg[:], ALU.mult)
@@ -235,9 +249,24 @@ def tile_list_elastography_line_scores_kernel(
         def make_h(k):
             kind, s = steps[k]
             if kind == "a":
-                make_h1(s)
+                make_h1(s, k % 2)
             else:
-                make_h2(s)
+                make_h2(s, k % 2)
+
+        def operand(width, name, pool_tag):
+            if pool_tag:
+                codes = ring.tile([P, width], U32, name=name + "c", tag=pool_tag[0], bufs=pool_tag[1], align_bytes=64)
+            else:
+                codes = keep.tile([P, width], U32, name=name + "c", align_bytes=64)
+            scales = keep.tile([P, width], U8, name=name + "s", align_bytes=64)
+            return codes, scales
+
+        def quantise(dst, c0, src):
+            w = src.shape[1] // PACK
+            nc.vector.quantize_mx(out=dst[0][:, c0 : c0 + w].bitcast(FP8X4), scales=dst[1][:, c0 : c0 + w], in_=src)
+
+        w3q = [operand(H, "w3q0", None)]
+        z0q = [operand(EARLY * P, "z0q0", None)]
 
         make_h(0)
         make_h(1)
@@ -270,117 +299,130 @@ def tile_list_elastography_line_scores_kernel(
                 load_plane(w4s, w4_scales)
                 w4w = [load_words(w4_words[a], "w4w%d" % a) for a in range(2)]
             if 10 <= k < 14:
-                for jt in (2 * (k - 10), 2 * (k - 10) + 1):
-                    turn_back(0, jt, zb0[:, jt, :])
+                turn_back(0, k - 10, zb0, 6)
+            if k == 8:
+                quantise(w3q[0], 0, w3g[0][:])
+            if k == 11:
+                quantise(z0q[0], 0, zb0[:, 0 : EARLY * KP])
             if k + 1 < len(steps) and steps[k + 1][0] == "b":
                 clamp_h2(steps[k + 1][1])
             if kind == "a":
                 scatter(pa[s % 2], idx3, h1[s], wg1t)
             else:
                 scatter(pb[s % (LEAD + 1)], idx4, h2[s], wg2t)
-        add_turned(SLICES - 1, pa[(SLICES - 1) % 2], False, True)
 
-        late = ring.tile([P, 3 * H], U32, name="late", tag="late", bufs=1, align_bytes=64)
-        late_s = keep.tile([P, 3 * H], U8, name="late_s", align_bytes=64)
-
-        def w3_cols(a, b, t):
-            c0 = a * H + b * KP + t * P
-            return slice(c0, c0 + P)
-
-        def quant_late(c0, src):
-            w = src.shape[1] // PACK
-            nc.vector.quantize_mx(out=late[:, c0 : c0 + w].bitcast(FP8X4), scales=late_s[:, c0 : c0 + w], in_=src)
-
-        zb0_flat = zb0[:].rearrange("p j c -> p (j c)")
-        quant_late(2 * H, zb0_flat[:, 0 : 4 * KP])
-        for b in range(2):
-            quant_late(b * KP, w3g[(0, b)][:])
-        for b in range(2):
-            quant_late(H + b * KP, w3g[(1, b)][:])
-        quant_late(2 * H + KP, zb0_flat[:, 4 * KP : 8 * KP])
+        late = operand(H + T2 - EARLY * P, "late", ("late", 1))
+        w3q.append((late[0][:, 0:H], late[1][:, 0:H]))
+        z0q.append((late[0][:, H:], late[1][:, H:]))
+        zb1 = ring.tile([P, JT * KP], BF16, name="zb1", tag="raw", bufs=3, align_bytes=64)
+        z1q = operand(T2, "z1q", ("raw", 3))
 
         acc3 = {}
-        z1 = {}
-        yq = {}
+        acc_bank = [0, 1, 2, 3, 0, 1, 2, 3, 0, 1, 2, 3, 4, 5, 0, 1]
 
         def product_pass(jt, b, a):
             if a == 0:
-                acc3[(jt, b)] = psum.tile([P, PACK, P], F32, name="acc3", tag="fw", bufs=4)
-                rhs = late[:, 2 * H + jt * P : 2 * H + (jt + 1) * P]
-                rhs_scale = late_s[:, 2 * H + jt * P : 2 * H + (jt + 1) * P]
+                acc3[(jt, b)] = bank(acc_bank[2 * jt + b], 1, [P, PACK, P], "acc3")
+                z, c0 = (z0q[0], jt * P) if jt < EARLY else (z0q[1], (jt - EARLY) * P)
             else:
-                rhs, rhs_scale = z1[jt][0][:], z1[jt][1][:]
+                z, c0 = z1q, jt * P
             for t in range(PACK):
-                cs = w3_cols(a, b, t)
+                cs = slice(b * KP + t * P, b * KP + (t + 1) * P)
                 nc.tensor.matmul_mx(
-                    out=acc3[(jt, b)][:, t, :], lhsT=late[:, cs].bitcast(FP8X4), lhsT_scale=late_s[:, cs],
-                    rhs=rhs.bitcast(FP8X4), rhs_scale=rhs_scale,
+                    out=acc3[(jt, b)][:, t, :], lhsT=w3q[a][0][:, cs].bitcast(FP8X4), lhsT_scale=w3q[a][1][:, cs],
+                    rhs=z[0][:, c0 : c0 + P].bitcast(FP8X4), rhs_scale=z[1][:, c0 : c0 + P],
                     start=(a == 0 and t == 0), stop=(a == 1 and t == PACK - 1),
                 )
 
-        def make_z1(jt):
-            zb = ring.tile([P, KP], BF16, name="zb1", tag="zb1", bufs=3, align_bytes=64)
-            turn_back(1, jt, zb[:])
-            codes = ring.tile([P, P], U32, name="z1c", tag="z1c", bufs=3, align_bytes=64)
-            scales = ring.tile([P, P], U8, name="z1s", tag="z1s", bufs=3, align_bytes=64)
-            nc.vector.quantize_mx(out=codes[:].bitcast(FP8X4), scales=scales[:], in_=zb[:])
-            z1[jt] = (codes, scales)
-
+        groups = [(0, 2), (2, 2), (4, 2), (6, 1), (7, 1)]
+        group_of = {}
+        for g, (j0, n) in enumerate(groups):
+            for u in range(n):
+                group_of[j0 + u] = (g, u)
         yb = {}
+        yq = {}
 
         def make_y(jt, b):
-            if b == 0:
-                yb[jt] = ring.tile([P, 2, KP], BF16, name="yb", tag="yb", bufs=2, align_bytes=64)
+            g, u = group_of[jt]
+            if b == 0 and u == 0:
+                yb[g] = ring.tile([P, 2 * groups[g][1] * KP], BF16, name="yb", tag="yb", bufs=2, align_bytes=64)
+            c0 = (b * groups[g][1] + u) * KP
             nc.vector.tensor_tensor(
-                yb[jt][:, b, :].rearrange("p (j t) -> p j t", t=PACK),
+                yb[g][:, c0 : c0 + KP].rearrange("p (j t) -> p j t", t=PACK),
                 acc3[(jt, b)][:].rearrange("p t j -> p j t"),
                 zf[(b, jt // 2)][:, jt % 2, :].rearrange("p (j t) -> p j t", t=PACK),
                 ALU.max,
             )
 
-        def quant_y(jt):
-            codes = ring.tile([P, 2 * P], U32, name="yc", tag="yc", bufs=2, align_bytes=64)
-            scales = ring.tile([P, 2 * P], U8, name="ys", tag="ys", bufs=2, align_bytes=64)
-            nc.vector.quantize_mx(
-                out=codes[:].bitcast(FP8X4), scales=scales[:], in_=yb[jt][:].rearrange("p b c -> p (b c)")
-            )
-            yq[jt] = (codes, scales)
+        def quant_y(g):
+            w = 2 * groups[g][1] * P
+            codes = ring.tile([P, w], U32, name="yc", tag="yc", bufs=2, align_bytes=64)
+            scales = ring.tile([P, w], U8, name="ys", tag="ys", bufs=2, align_bytes=64)
+            yq[g] = (codes, scales)
+            quantise(yq[g], 0, yb[g][:])
 
-        def scores(jt):
-            codes, scales = yq[jt]
-            acc = psum.tile([P, N // P, P], F32, name="o_ps", tag="hb", bufs=2)
+        def scores(g):
+            j0, n_jt = groups[g]
+            w = n_jt * P
+            codes, scales = yq[g]
+            if n_jt == 2:
+                acc = bank(6, 2, [P, 4, w], "o_ps")
+            else:
+                acc = bank(6 + j0 % 2, 1, [P, 4, w], "o_ps")
             for n in range(N // P):
                 for b in range(2):
                     nc.tensor.matmul_mx(
                         out=acc[:, n, :], lhsT=w4w[b][:, n * P : (n + 1) * P].bitcast(FP8X4),
                         lhsT_scale=w4s[4 * b : P, n * P : (n + 1) * P],
-                        rhs=codes[:, b * P : (b + 1) * P].bitcast(FP8X4), rhs_scale=scales[:, b * P : (b + 1) * P],
+                        rhs=codes[:, b * w : (b + 1) * w].bitcast(FP8X4), rhs_scale=scales[:, b * w : (b + 1) * w],
                         start=(b == 0), stop=(b == 1),
                     )
-            res = ring.tile([P, N // P, P], F32, name="res", tag="res", bufs=3)
-            nc.scalar.copy(res[:], acc[:])
+            res = ring.tile([P, N // P, w], F32, name="res", tag="res", bufs=3)
+            if n_jt == 2:
+                nc.scalar.copy(res[:, 0:2, :], acc[:, 0:2, :])
+                nc.scalar.copy(res[:, 2, :], acc[:, 2, :])
+            else:
+                nc.scalar.copy(res[:], acc[:, 0:3, :])
             nc.sync.dma_start(
-                out=out[:, jt * P : (jt + 1) * P].rearrange("(n p) j -> p n j", p=P), in_=res[:]
+                out=out[:, j0 * P : j0 * P + w].rearrange("(n p) j -> p n j", p=P), in_=res[:]
             )
+
+        def quant_z1(j0, n):
+            quantise(z1q, j0 * P, zb1[:, j0 * KP : (j0 + n) * KP])
 
         for jt in range(2):
             for b in range(2):
                 product_pass(jt, b, 0)
-        make_z1(0)
-        make_z1(1)
+        add_turned(SLICES - 1, pa[(SLICES - 1) % 2], False, True)
+        quantise(w3q[1], 0, w3g[1][:])
+        quantise(z0q[1], 0, zb0[:, EARLY * KP : (EARLY + 2) * KP])
+        quantise(z0q[1], 2 * P, zb0[:, (EARLY + 2) * KP : JT * KP])
+        turn_back(1, 0, zb1, 6)
+        turn_back(1, 1, zb1, 4)
+        quant_z1(0, 1)
+        for b in range(2):
+            product_pass(0, b, 1)
+        quant_z1(1, 1)
         for jt in range(JT):
-            for b in range(2):
-                product_pass(jt, b, 1)
-            if jt + 2 < JT:
-                make_z1(jt + 2)
+            if jt == 0:
+                turn_back(1, 2, zb1, 6)
+            if jt == 2:
+                turn_back(1, 3, zb1, 4)
+            if jt + 1 < JT:
+                for b in range(2):
+                    product_pass(jt + 1, b, 1)
             make_y(jt, 0)
-            if jt >= 1:
-                quant_y(jt - 1)
+            if jt + 2 < JT:
+                product_pass(jt + 2, 0, 0)
+            done = [g for g, (j0, n) in enumerate(groups) if j0 + n == jt]
+            for g in done:
+                quant_y(g)
+            if jt in (0, 2, 4):
+                quant_z1(jt + 2, 2)
             make_y(jt, 1)
             if jt + 2 < JT:
-                for b in range(2):
-                    product_pass(jt + 2, b, 0)
-            if jt >= 1:
-                scores(jt - 1)
-        quant_y(JT - 1)
-        scores(JT - 1)
+                product_pass(jt + 2, 1, 0)
+            for g in done:
+                scores(g)
+        quant_y(len(groups) - 1)
+        scores(len(groups) - 1)

@@ -22,8 +22,10 @@ PACK = 4
 KP = P * PACK
 SLICES = H // P
 JT = T2 // P
-W1_CHUNK = 256
+W1_CHUNKS = [(0, 3), (3, 3), (6, 2)]
 LEAD = 3
+PAGES = 3
+PAGE_BYTES = 4 * T2
 BANK_BYTES = 2048
 EARLY = 2
 
@@ -37,6 +39,7 @@ def tile_list_elastography_line_scores_kernel(
         lists = ctx.enter_context(tc.tile_pool(name="lists", bufs=1))
         keep = ctx.enter_context(tc.tile_pool(name="keep", bufs=1))
         ring = ctx.enter_context(tc.tile_pool(name="ring", bufs=1))
+        reuse = ctx.enter_context(tc.tile_pool(name="reuse", bufs=1))
         psum = ctx.enter_context(tc.psum_pool(name="psum", bufs=1))
 
         def bank(first, count, shape, name):
@@ -60,8 +63,11 @@ def tile_list_elastography_line_scores_kernel(
                     in_=scales[:, 4 * q : 4 * q + 4, :].bitcast(I32),
                 )
 
-        def load_words(words, name):
-            t = keep.tile([P, words.shape[1]], I32, name=name, align_bytes=64)
+        def load_words(words, name, offset=None):
+            if offset is None:
+                t = keep.tile([P, words.shape[1]], I32, name=name, align_bytes=64)
+            else:
+                t = reuse.tile([P, words.shape[1]], I32, name=name, offset=offset)
             nc.sync.dma_start(out=t[:], in_=words.rearrange("p t i -> p (t i)").bitcast(I32))
             return t
 
@@ -80,30 +86,32 @@ def tile_list_elastography_line_scores_kernel(
         make_identity(nc, ident[:])
 
         t1s = zeroed_plane(T, "t1s")
-        t2w = load_words(tab2_words[0], "t2w")
+        t2w = load_words(tab2_words[0], "t2w", PAGE_BYTES - 32)
         load_plane(t2s, tab2_scales)
         idx2 = load_list(offs2, "idx2")
         w2w = keep.tile([P, 2 * H], U8, name="w2w", align_bytes=64)
         nc.sync.dma_start(out=w2w[:].bitcast(I32), in_=w2_words[0].bitcast(I32))
         load_plane(w2s, w2_scales)
         idx4 = load_list(offs4, "idx4")
-        wg2t = keep.tile([P, S], F32, name="wg2t")
+        wg2t = ring.tile([P, S], F32, name="wg2t", tag="later", bufs=1, align_bytes=64)
         nc.sync.dma_start(out=wg2t[:], in_=wg2)
         t1w = [load_words(tab_words[0], "t1w0")]
         idx1 = load_list(offs, "idx1")
         t1w.append(load_words(tab_words[1], "t1w1"))
         load_plane(t1s, tab_scales)
 
-        pb = []
-        for i in range(LEAD + 1):
-            page = keep.tile([P, T2], F32, name="pb%d" % i)
+        def page_now(name):
+            page = keep.tile([P, T2], F32, name=name)
             nc.vector.memset(page[:].bitcast(I32), 0)
-            pb.append(page)
-        pa = []
-        for i in range(2):
-            page = keep.tile([P, T2], F32, name="pa%d" % i)
-            nc.vector.memset(page[:].bitcast(I32), 0)
-            pa.append(page)
+            return page
+
+        def page_later(name, slot):
+            page = reuse.tile([P, T2], F32, name=name, offset=slot * PAGE_BYTES)
+            nc.gpsimd.memset(page[:].bitcast(I32), 0)
+            return page
+
+        pb = [page_now("pb0"), page_now("pb1")]
+        pa_last = page_now("pa2")
         w4s = keep.tile([P, N], U8, name="w4s", align_bytes=64)
         nc.gpsimd.memset(w4s[:].bitcast(I32), 0)
 
@@ -114,32 +122,35 @@ def tile_list_elastography_line_scores_kernel(
 
         v2s = gather(t2s[:], U8, idx2, "v2s")
         v2w = gather(t2w[:].bitcast(U32), U32, idx2, "v2w")
+        pb.append(page_later("pb2", 0))
+        pa = [page_later("pa0", 1), page_later("pa1", 2), pa_last]
 
         w1c = keep.tile([P, 2 * H], U32, name="w1c", align_bytes=64)
         w1s = keep.tile([P, 2 * H], U8, name="w1s", align_bytes=64)
 
-        def w1_chunk(c):
-            cs = slice(c * W1_CHUNK, (c + 1) * W1_CHUNK)
-            tag = "hold" if c == 0 else "grp1"
-            grp = ring.tile([P, 2 * W1_CHUNK * PACK], BF16, name="grp1", tag=tag, bufs=1, align_bytes=64)
-            for a in range(2):
-                raw = ring.tile([P, PACK, W1_CHUNK], F32, name="raw1", tag="raw", bufs=3, align_bytes=64)
-                nc.sync.dma_start(
-                    out=raw[:], in_=w1[a * KP : (a + 1) * KP, cs].rearrange("(p j) c -> p j c", j=PACK)
-                )
-                nc.scalar.copy(
-                    grp[:, a * W1_CHUNK * PACK : (a + 1) * W1_CHUNK * PACK].rearrange(
-                        "p (c i j) -> p c j i", i=4, j=PACK
-                    ),
-                    raw[:].rearrange("p j (c i) -> p c j i", i=4),
-                )
-            both = slice(2 * c * W1_CHUNK, 2 * (c + 1) * W1_CHUNK)
-            nc.vector.quantize_mx(out=w1c[:, both].bitcast(FP8X4), scales=w1s[:, both], in_=grp[:])
+        w1g = {}
+
+        def w1_cast(c, a):
+            s0, n = W1_CHUNKS[c]
+            width = n * P
+            if a == 0:
+                tag = "hold" if c == 0 else "grp1"
+                w1g[c] = ring.tile([P, 2 * width * PACK], BF16, name="grp1", tag=tag, bufs=1, align_bytes=64)
+            raw = ring.tile([P, PACK, width], F32, name="raw1", tag="raw", bufs=3, align_bytes=64)
+            nc.sync.dma_start(
+                out=raw[:],
+                in_=w1[a * KP : (a + 1) * KP, s0 * P : s0 * P + width].rearrange("(p j) c -> p j c", j=PACK),
+            )
+            grouped = w1g[c][:, a * width * PACK : (a + 1) * width * PACK]
+            nc.scalar.copy(
+                grouped.rearrange("p (c i j) -> p c j i", i=4, j=PACK),
+                raw[:].rearrange("p j (c i) -> p c j i", i=4),
+            )
+            cs = slice(a * H + s0 * P, a * H + s0 * P + width)
+            nc.vector.quantize_mx(out=w1c[:, cs].bitcast(FP8X4), scales=w1s[:, cs], in_=grouped)
 
         def w1_cols(a, s):
-            c, half = divmod(s, 2)
-            c0 = (2 * c + a) * W1_CHUNK + half * P
-            return slice(c0, c0 + P)
+            return slice(a * H + s * P, a * H + (s + 1) * P)
 
         w3g = {}
 
@@ -152,8 +163,8 @@ def tile_list_elastography_line_scores_kernel(
             if b == 0:
                 w3g[a] = keep.tile([P, 2 * KP * PACK], BF16, name="w3g%d" % a, align_bytes=64)
             nc.scalar.copy(
-                w3g[a][:, b * KP * PACK : (b + 1) * KP * PACK].rearrange("p (t q j) -> p q j t", t=PACK, j=PACK),
-                raw[:].rearrange("p j (q t) -> p q j t", t=PACK),
+                w3g[a][:, b * KP * PACK : (b + 1) * KP * PACK].rearrange("p (t q j) -> p q t j", t=PACK, j=PACK),
+                raw[:].rearrange("p j (q t) -> p q t j", t=PACK),
             )
 
         h1 = {}
@@ -172,8 +183,8 @@ def tile_list_elastography_line_scores_kernel(
                 start=True, stop=True,
             )
             h = ring.tile([P, S], F32, name="h2", tag="h", bufs=4)
-            if s == 0:
-                nc.vector.tensor_scalar(h[:], acc[:], cols[:, 0:1], None, ALU.max)
+            if s < 2:
+                nc.vector.tensor_scalar(h[:], acc[:], cols[:, s : s + 1], None, ALU.max)
             else:
                 nc.scalar.copy(h[:], acc[:])
             h2[s] = h
@@ -241,10 +252,9 @@ def tile_list_elastography_line_scores_kernel(
             nc.vector.tensor_tensor(page[:].indirect(idx[:]), h[:], wg[:], ALU.mult)
 
         steps = [("b", s) for s in range(LEAD)]
-        for s in range(SLICES):
-            steps.append(("a", s))
-            if s + LEAD < SLICES:
-                steps.append(("b", s + LEAD))
+        steps.extend([("a", s) for s in range(LEAD)])
+        for s in range(LEAD, SLICES):
+            steps.extend([("b", s), ("a", s)])
 
         def make_h(k):
             kind, s = steps[k]
@@ -265,12 +275,32 @@ def tile_list_elastography_line_scores_kernel(
             w = src.shape[1] // PACK
             nc.vector.quantize_mx(out=dst[0][:, c0 : c0 + w].bitcast(FP8X4), scales=dst[1][:, c0 : c0 + w], in_=src)
 
-        w3q = [operand(H, "w3q0", None)]
         z0q = [operand(EARLY * P, "z0q0", None)]
+
+        page_of = {"a": pa, "b": pb}
+        placed = set()
+        added = set()
+
+        def add_ready():
+            for s in range(SLICES):
+                if s >= 2 and ("a", s - 2) not in added:
+                    continue
+                if ("base", s) not in added and s in base_t:
+                    add_turned(s, base_t[s], True, False)
+                    added.add(("base", s))
+                for kind in ("b", "a"):
+                    if ("base", s) in added and (kind, s) in placed and (kind, s) not in added:
+                        add_turned(s, page_of[kind][s % PAGES], False, kind == "a")
+                        added.add((kind, s))
+
+        base_at = {1: [0, 1], 2: [2], 3: [3], 4: [4], 6: [5], 8: [6], 10: [7]}
+        w1_at = {2: [(1, 0)], 3: [(1, 1)], 4: [(2, 0)], 5: [(2, 1)]}
+        w3_at = {6: (0, 0), 7: (0, 1), 12: (1, 0), 14: (1, 1)}
 
         make_h(0)
         make_h(1)
-        w1_chunk(0)
+        w1_cast(0, 0)
+        w1_cast(0, 1)
         idx3 = load_list(offs3, "idx3")
         wg1t = ring.tile([P, S], F32, name="wg1t", tag="late", bufs=1, align_bytes=64)
         nc.sync.dma_start(out=wg1t[:], in_=wg1)
@@ -281,35 +311,30 @@ def tile_list_elastography_line_scores_kernel(
                 v1s = gather(t1s[:], U8, idx1, "v1s")
             if k + 2 < len(steps):
                 make_h(k + 2)
-            if k >= 1 and steps[k - 1][0] == "a":
-                add_turned(steps[k - 1][1], pa[steps[k - 1][1] % 2], False, True)
-            if k in (1, 3, 5):
-                w1_chunk(k // 2 + 1)
-            if k in (2, 4, 6, 7):
-                i = (2, 4, 6, 7).index(k)
-                w3_cast(i // 2, i % 2)
-            if k == 1:
-                load_base(0)
-            if kind == "a":
-                if s + 1 < SLICES:
-                    load_base(s + 1)
-                add_turned(s, base_t[s], True, False)
-                add_turned(s, pb[s % (LEAD + 1)], False, False)
+            add_ready()
+            for c, a in w1_at.get(k, []):
+                w1_cast(c, a)
+            for sb in base_at.get(k, []):
+                load_base(sb)
+            if k in w3_at:
+                w3_cast(w3_at[k][0], w3_at[k][1])
             if k == 8:
                 load_plane(w4s, w4_scales)
                 w4w = [load_words(w4_words[a], "w4w%d" % a) for a in range(2)]
-            if 10 <= k < 14:
-                turn_back(0, k - 10, zb0, 6)
-            if k == 8:
-                quantise(w3q[0], 0, w3g[0][:])
-            if k == 11:
+            if 8 <= k < 12:
+                turn_back(0, k - 8, zb0, 6)
+            if k == 10:
                 quantise(z0q[0], 0, zb0[:, 0 : EARLY * KP])
-            if k + 1 < len(steps) and steps[k + 1][0] == "b":
+            if k == len(steps) - 1:
+                w3q = [operand(H, "w3q0", ("later", 1))]
+                quantise(w3q[0], 0, w3g[0][:])
+            if k + 1 < len(steps) and steps[k + 1][0] == "b" and steps[k + 1][1] >= 2:
                 clamp_h2(steps[k + 1][1])
             if kind == "a":
-                scatter(pa[s % 2], idx3, h1[s], wg1t)
+                scatter(pa[s % PAGES], idx3, h1[s], wg1t)
             else:
-                scatter(pb[s % (LEAD + 1)], idx4, h2[s], wg2t)
+                scatter(pb[s % PAGES], idx4, h2[s], wg2t)
+            placed.add((kind, s))
 
         late = operand(H + T2 - EARLY * P, "late", ("late", 1))
         w3q.append((late[0][:, 0:H], late[1][:, 0:H]))
@@ -393,7 +418,7 @@ def tile_list_elastography_line_scores_kernel(
         for jt in range(2):
             for b in range(2):
                 product_pass(jt, b, 0)
-        add_turned(SLICES - 1, pa[(SLICES - 1) % 2], False, True)
+        add_ready()
         quantise(w3q[1], 0, w3g[1][:])
         quantise(z0q[1], 0, zb0[:, EARLY * KP : (EARLY + 2) * KP])
         quantise(z0q[1], 2 * P, zb0[:, (EARLY + 2) * KP : JT * KP])

@@ -86,17 +86,17 @@ def tile_list_elastography_line_scores_kernel(
         make_identity(nc, ident[:])
 
         t1s = zeroed_plane(T, "t1s")
-        t2w = load_words(tab2_words[0], "t2w", PAGE_BYTES - 32)
+        t2w = load_words(tab2_words[0], "t2w")
         load_plane(t2s, tab2_scales)
         idx2 = load_list(offs2, "idx2")
+        idx1 = load_list(offs, "idx1")
+        t1w = [load_words(tab_words[0], "t1w0", PAGE_BYTES - 32)]
         w2w = keep.tile([P, 2 * H], U8, name="w2w", align_bytes=64)
         nc.sync.dma_start(out=w2w[:].bitcast(I32), in_=w2_words[0].bitcast(I32))
         load_plane(w2s, w2_scales)
         idx4 = load_list(offs4, "idx4")
         wg2t = ring.tile([P, S], F32, name="wg2t", tag="later", bufs=1, align_bytes=64)
         nc.sync.dma_start(out=wg2t[:], in_=wg2)
-        t1w = [load_words(tab_words[0], "t1w0")]
-        idx1 = load_list(offs, "idx1")
         t1w.append(load_words(tab_words[1], "t1w1"))
         load_plane(t1s, tab_scales)
 
@@ -122,6 +122,7 @@ def tile_list_elastography_line_scores_kernel(
 
         v2s = gather(t2s[:], U8, idx2, "v2s")
         v2w = gather(t2w[:].bitcast(U32), U32, idx2, "v2w")
+        v1w = [gather(t1w[0][:].bitcast(U32), U32, idx1, "v1w0")]
         pb.append(page_later("pb2", 0))
         pa = [page_later("pa0", 1), page_later("pa1", 2), pa_last]
 
@@ -154,17 +155,24 @@ def tile_list_elastography_line_scores_kernel(
 
         w3g = {}
 
-        def w3_cast(a, b):
-            raw = ring.tile([P, PACK, KP], F32, name="raw3", tag="raw", bufs=3, align_bytes=64)
-            nc.sync.dma_start(
-                out=raw[:],
-                in_=w3[a * KP : (a + 1) * KP, b * KP : (b + 1) * KP].rearrange("(p j) c -> p j c", j=PACK),
-            )
-            if b == 0:
-                w3g[a] = keep.tile([P, 2 * KP * PACK], BF16, name="w3g%d" % a, align_bytes=64)
+        w3raw = {}
+
+        def w3_cast(a, b, half):
+            if half == 0:
+                raw = ring.tile([P, PACK, KP], F32, name="raw3", tag="raw", bufs=3, align_bytes=64)
+                nc.sync.dma_start(
+                    out=raw[:],
+                    in_=w3[a * KP : (a + 1) * KP, b * KP : (b + 1) * KP].rearrange("(p j) c -> p j c", j=PACK),
+                )
+                w3raw[(a, b)] = raw
+                if b == 0:
+                    w3g[a] = keep.tile([P, 2 * KP * PACK], BF16, name="w3g%d" % a, align_bytes=64)
+            qs = slice(half * P // 2, (half + 1) * P // 2)
             nc.scalar.copy(
-                w3g[a][:, b * KP * PACK : (b + 1) * KP * PACK].rearrange("p (t q j) -> p q t j", t=PACK, j=PACK),
-                raw[:].rearrange("p j (q t) -> p q t j", t=PACK),
+                w3g[a][:, b * KP * PACK : (b + 1) * KP * PACK].rearrange(
+                    "p (t q j) -> p q t j", t=PACK, j=PACK
+                )[:, qs, :, :],
+                w3raw[(a, b)][:].rearrange("p j (q t) -> p q t j", t=PACK)[:, qs, :, :],
             )
 
         h1 = {}
@@ -173,27 +181,25 @@ def tile_list_elastography_line_scores_kernel(
         fw = {}
         zt = {}
         zf = {}
-        zb0 = keep.tile([P, JT * KP], BF16, name="zb0", align_bytes=64)
+        zf0 = keep.tile([P, JT * KP], F32, name="zf0")
+        zb0 = keep.tile([P, EARLY * KP], BF16, name="zb0", align_bytes=64)
+
+        h2_ps = {}
 
         def make_h2(s, b):
-            acc = bank(b, 1, [P, S], "h2_ps")
+            h2_ps[s] = bank(b, 1, [P, S], "h2_ps")
             nc.tensor.matmul_mx(
-                out=acc[:], lhsT=w2w[:, 2 * P * s : 2 * P * (s + 1)].bitcast(FP4X4),
+                out=h2_ps[s][:], lhsT=w2w[:, 2 * P * s : 2 * P * (s + 1)].bitcast(FP4X4),
                 lhsT_scale=w2s[:, P * s : P * (s + 1)], rhs=v2w[:].bitcast(FP8X4), rhs_scale=v2s[:],
                 start=True, stop=True,
             )
-            h = ring.tile([P, S], F32, name="h2", tag="h", bufs=4)
-            if s < 2:
-                nc.vector.tensor_scalar(h[:], acc[:], cols[:, s : s + 1], None, ALU.max)
-            else:
-                nc.scalar.copy(h[:], acc[:])
-            h2[s] = h
 
         def clamp_h2(s):
-            src = h2[s]
             if s == LEAD - 1:
                 h2[s] = ring.tile([P, S], F32, name="h2_held", tag="hold", bufs=1, align_bytes=64)
-            nc.vector.tensor_scalar(h2[s][:], src[:], cols[:, s : s + 1], None, ALU.max)
+            else:
+                h2[s] = ring.tile([P, S], F32, name="h2", tag="h", bufs=4)
+            nc.vector.tensor_scalar(h2[s][:], h2_ps[s][:], cols[:, s : s + 1], None, ALU.max)
 
         def make_h1(s, b):
             acc = bank(b, 1, [P, S], "h1_ps")
@@ -203,7 +209,10 @@ def tile_list_elastography_line_scores_kernel(
                     lhsT_scale=w1s[:, w1_cols(a, s)], rhs=v1w[a][:].bitcast(FP8X4),
                     rhs_scale=v1s[4 * a : P, :], start=(a == 0), stop=(a == 1),
                 )
-            h = ring.tile([P, S], F32, name="h1", tag="h", bufs=4)
+            if s == SLICES - 1:
+                h = ring.tile([P, S], F32, name="h1_last", tag="latest", bufs=1, align_bytes=64)
+            else:
+                h = ring.tile([P, S], F32, name="h1", tag="h", bufs=4)
             nc.scalar.activation(h[:], acc[:], ACT.Tanh)
             nc.scalar.activation(h[:], h[:], ACT.Copy, scale=cols[:, SLICES + s : SLICES + s + 1])
             h1[s] = h
@@ -226,7 +235,7 @@ def tile_list_elastography_line_scores_kernel(
                 if last:
                     a, quarter = divmod(s, 4)
                     if quarter == 0:
-                        zt[(a, half)] = ring.tile([P, 4, PACK, P], F32, name="zt", tag="zt", bufs=3)
+                        zt[(a, half)] = ring.tile([P, 4, PACK, P], F32, name="zt", tag="zt", bufs=4)
                     nc.scalar.copy(
                         zt[(a, half)][:, :, :, 32 * quarter : 32 * (quarter + 1)],
                         fw[(s, half)][:].rearrange("j g (q t) -> j g t q", t=PACK),
@@ -235,7 +244,7 @@ def tile_list_elastography_line_scores_kernel(
         def turn_back(a, pair, zb, first_bank):
             banks = bank(first_bank, 2, [P, 2, PACK, P], "bk")
             if a == 0:
-                zf[(a, pair)] = keep.tile([P, 2, KP], F32, name="zf0%d" % pair)
+                zf[(a, pair)] = zf0[:, 2 * pair * KP : 2 * (pair + 1) * KP].rearrange("p (u c) -> p u c", u=2)
             else:
                 zf[(a, pair)] = ring.tile([P, 2, KP], F32, name="zf1", tag="base", bufs=4)
             for u in range(2):
@@ -245,7 +254,8 @@ def tile_list_elastography_line_scores_kernel(
             for u in range(2):
                 jt = 2 * pair + u
                 woven = banks[:, u, :, :].rearrange("p t j -> p j t")
-                nc.scalar.copy(zb[:, jt * KP : (jt + 1) * KP].rearrange("p (j t) -> p j t", t=PACK), woven)
+                if a == 1 or jt < EARLY:
+                    nc.scalar.copy(zb[:, jt * KP : (jt + 1) * KP].rearrange("p (j t) -> p j t", t=PACK), woven)
                 nc.scalar.copy(zf[(a, pair)][:, u, :].rearrange("p (j t) -> p j t", t=PACK), woven)
 
         def scatter(page, idx, h, wg):
@@ -295,9 +305,12 @@ def tile_list_elastography_line_scores_kernel(
 
         base_at = {1: [0, 1], 2: [2], 3: [3], 4: [4], 6: [5], 8: [6], 10: [7]}
         w1_at = {2: [(1, 0)], 3: [(1, 1)], 4: [(2, 0)], 5: [(2, 1)]}
-        w3_at = {6: (0, 0), 7: (0, 1), 12: (1, 0), 14: (1, 1)}
+        w3_at = {6: [(0, 0, 0), (0, 0, 1)], 7: [(0, 1, 0)], 9: [(0, 1, 1)], 10: [(1, 0, 0)], 11: [(1, 0, 1)],
+                 13: [(1, 1, 0)], 14: [(1, 1, 1)]}
+        back_at = {8: 0, 9: 1, 11: 2, 12: 3}
 
         make_h(0)
+        clamp_h2(0)
         make_h(1)
         w1_cast(0, 0)
         w1_cast(0, 1)
@@ -307,7 +320,7 @@ def tile_list_elastography_line_scores_kernel(
         for k in range(len(steps)):
             kind, s = steps[k]
             if k == 1:
-                v1w = [gather(t1w[a][:].bitcast(U32), U32, idx1, "v1w%d" % a) for a in range(2)]
+                v1w.append(gather(t1w[1][:].bitcast(U32), U32, idx1, "v1w1"))
                 v1s = gather(t1s[:], U8, idx1, "v1s")
             if k + 2 < len(steps):
                 make_h(k + 2)
@@ -316,19 +329,19 @@ def tile_list_elastography_line_scores_kernel(
                 w1_cast(c, a)
             for sb in base_at.get(k, []):
                 load_base(sb)
-            if k in w3_at:
-                w3_cast(w3_at[k][0], w3_at[k][1])
+            for a, b, half in w3_at.get(k, []):
+                w3_cast(a, b, half)
             if k == 8:
                 load_plane(w4s, w4_scales)
                 w4w = [load_words(w4_words[a], "w4w%d" % a) for a in range(2)]
-            if 8 <= k < 12:
-                turn_back(0, k - 8, zb0, 6)
+            if k in back_at:
+                turn_back(0, back_at[k], zb0, 6)
             if k == 10:
                 quantise(z0q[0], 0, zb0[:, 0 : EARLY * KP])
             if k == len(steps) - 1:
                 w3q = [operand(H, "w3q0", ("later", 1))]
                 quantise(w3q[0], 0, w3g[0][:])
-            if k + 1 < len(steps) and steps[k + 1][0] == "b" and steps[k + 1][1] >= 2:
+            if k + 1 < len(steps) and steps[k + 1][0] == "b":
                 clamp_h2(steps[k + 1][1])
             if kind == "a":
                 scatter(pa[s % PAGES], idx3, h1[s], wg1t)
@@ -419,9 +432,11 @@ def tile_list_elastography_line_scores_kernel(
             for b in range(2):
                 product_pass(jt, b, 0)
         add_ready()
+        zb0_late = ring.tile([P, (JT - EARLY) * KP], BF16, name="zb0_late", tag="latest", bufs=1, align_bytes=64)
+        nc.vector.tensor_copy(zb0_late[:], zf0[:, EARLY * KP : JT * KP])
         quantise(w3q[1], 0, w3g[1][:])
-        quantise(z0q[1], 0, zb0[:, EARLY * KP : (EARLY + 2) * KP])
-        quantise(z0q[1], 2 * P, zb0[:, (EARLY + 2) * KP : JT * KP])
+        quantise(z0q[1], 0, zb0_late[:, 0 : 2 * KP])
+        quantise(z0q[1], 2 * P, zb0_late[:, 2 * KP : 6 * KP])
         turn_back(1, 0, zb1, 6)
         turn_back(1, 1, zb1, 4)
         quant_z1(0, 1)

from contextlib import ExitStack

import concourse.mybir as mybir
from concourse.masks import make_identity

K, K2, T, S, H, N, T2 = 1024, 512, 2048, 512, 1024, 384, 1024
FLOPS = 2 * (K * H * S + K2 * H * S + H * H * T2 + H * N * T2)

F32 = mybir.dt.float32
BF16 = mybir.dt.bfloat16
I32 = mybir.dt.int32
U32 = mybir.dt.uint32
U16 = mybir.dt.uint16
U8 = mybir.dt.uint8
FP8X4 = mybir.dt.float8_e4m3fn_x4
FP4X4 = mybir.dt.float4_e2m1fn_x4
ALU = mybir.AluOpType
ACT = mybir.ActivationFunctionType

P = 128
PACK = 4
KP = P * PACK
SLICES = H // P
JT = T2 // P
W1_CHUNKS = [(0, 3), (3, 3), (6, 2)]
LEAD = 3
PAGES = 3
PAGE_BYTES = 4 * T2
BANK_BYTES = 2048
EARLY = 2


def tile_list_elastography_line_scores_kernel(
    tc, tab_words, tab_scales, tab2_words, tab2_scales, offs, offs2, offs3, offs4,
    w1, gain1, w2_words, w2_scales, low2, wg1, wg2, base, w3, w4_words, w4_scales, out,
):
    nc = tc.nc
    with ExitStack() as ctx:
        lists = ctx.enter_context(tc.tile_pool(name="lists", bufs=1))
        keep = ctx.enter_context(tc.tile_pool(name="keep", bufs=1))
        ring = ctx.enter_context(tc.tile_pool(name="ring", bufs=1))
        reuse = ctx.enter_context(tc.tile_pool(name="reuse", bufs=1))
        psum = ctx.enter_context(tc.psum_pool(name="psum", bufs=1))

        def bank(first, count, shape, name):
            return psum.tile(shape, F32, name=name, tag="bank%d_%d" % (first, count), bufs=1, offset=first * BANK_BYTES)

        def load_list(src, name):
            t = lists.tile([P, S // 16], U16, name=name)
            nc.sync.dma_start(t[:], src)
            return t

        def zeroed_plane(width, name):
            t = keep.tile([P, width], U8, name=name, align_bytes=64)
            nc.vector.memset(t[:].bitcast(I32), 0)
            return t

        def load_plane(t, scales):
            passes = scales.shape[0]
            for q in range(4):
                nc.sync.dma_start(
                    out=t[32 * q : 32 * q + 4 * passes, :].bitcast(I32),
                    in_=scales[:, 4 * q : 4 * q + 4, :].bitcast(I32),
                )

        def load_words(words, name, offset=None):
            if offset is None:
                t = keep.tile([P, words.shape[1]], I32, name=name, align_bytes=64)
            else:
                t = reuse.tile([P, words.shape[1]], I32, name=name, offset=offset)
            nc.sync.dma_start(out=t[:], in_=words.rearrange("p t i -> p (t i)").bitcast(I32))
            return t

        def gather(window, dtype, idx, name):
            g = keep.tile([P, S], dtype, name=name, align_bytes=64)
            nc.vector.tensor_copy(g[:], window.indirect(idx[:]))
            return g

        t2s = zeroed_plane(T, "t2s")
        w2s = zeroed_plane(H, "w2s")
        vec = keep.tile([P, P], F32, name="vec")
        nc.gpsimd.memset(vec[:], 0.0)
        nc.gpsimd.dma_start(out=vec[0:SLICES, :], in_=low2.rearrange("(s p) -> s p", p=P))
        nc.gpsimd.dma_start(out=vec[SLICES : 2 * SLICES, :], in_=gain1.rearrange("(s p) -> s p", p=P))
        ident = keep.tile([P, P], F32, name="ident")
        make_identity(nc, ident[:])

        t1s = zeroed_plane(T, "t1s")
        t2w = load_words(tab2_words[0], "t2w")
        load_plane(t2s, tab2_scales)
        idx2 = load_list(offs2, "idx2")
        idx1 = load_list(offs, "idx1")
        t1w = [load_words(tab_words[0], "t1w0", PAGE_BYTES - 32)]
        w2w = keep.tile([P, 2 * H], U8, name="w2w", align_bytes=64)
        nc.sync.dma_start(out=w2w[:].bitcast(I32), in_=w2_words[0].bitcast(I32))
        load_plane(w2s, w2_scales)
        idx4 = load_list(offs4, "idx4")
        wg2t = ring.tile([P, S], F32, name="wg2t", tag="later", bufs=1, align_bytes=64)
        nc.sync.dma_start(out=wg2t[:], in_=wg2)
        t1w.append(load_words(tab_words[1], "t1w1"))
        load_plane(t1s, tab_scales)

        def page_now(name):
            page = keep.tile([P, T2], F32, name=name)
            nc.vector.memset(page[:].bitcast(I32), 0)
            return page

        def page_later(name, slot):
            page = reuse.tile([P, T2], F32, name=name, offset=slot * PAGE_BYTES)
            nc.gpsimd.memset(page[:].bitcast(I32), 0)
            return page

        pb = [page_now("pb0"), page_now("pb1")]
        pa_last = page_now("pa2")
        w4s = keep.tile([P, N], U8, name="w4s", align_bytes=64)
        nc.gpsimd.memset(w4s[:].bitcast(I32), 0)

        vec_ps = bank(7, 1, [P, KP], "vec_ps")
        nc.tensor.transpose(vec_ps[:, 0:P], vec[:], ident[:])
        cols = keep.tile([P, 2 * SLICES], F32, name="cols")
        nc.scalar.copy(cols[:], vec_ps[:, 0 : 2 * SLICES])

        v2s = gather(t2s[:], U8, idx2, "v2s")
        v2w = gather(t2w[:].bitcast(U32), U32, idx2, "v2w")
        v1w = [gather(t1w[0][:].bitcast(U32), U32, idx1, "v1w0")]
        pb.append(page_later("pb2", 0))
        pa = [page_later("pa0", 1), page_later("pa1", 2), pa_last]

        w1c = keep.tile([P, 2 * H], U32, name="w1c", align_bytes=64)
        w1s = keep.tile([P, 2 * H], U8, name="w1s", align_bytes=64)

        w1g = {}

        def w1_cast(c, a):
            s0, n = W1_CHUNKS[c]
            width = n * P
            if a == 0:
                tag = "hold" if c == 0 else "grp1"
                w1g[c] = ring.tile([P, 2 * width * PACK], BF16, name="grp1", tag=tag, bufs=1, align_bytes=64)
            raw = ring.tile([P, PACK, width], F32, name="raw1", tag="raw", bufs=3, align_bytes=64)
            nc.sync.dma_start(
                out=raw[:],
                in_=w1[a * KP : (a + 1) * KP, s0 * P : s0 * P + width].rearrange("(p j) c -> p j c", j=PACK),
            )
            grouped = w1g[c][:, a * width * PACK : (a + 1) * width * PACK]
            nc.scalar.copy(
                grouped.rearrange("p (c i j) -> p c j i", i=4, j=PACK),
                raw[:].rearrange("p j (c i) -> p c j i", i=4),
            )
            cs = slice(a * H + s0 * P, a * H + s0 * P + width)
            nc.vector.quantize_mx(out=w1c[:, cs].bitcast(FP8X4), scales=w1s[:, cs], in_=grouped)

        def w1_cols(a, s):
            return slice(a * H + s * P, a * H + (s + 1) * P)

        w3g = {}

        w3raw = {}

        def w3_cast(a, b, half):
            if half == 0:
                raw = ring.tile([P, PACK, KP], F32, name="raw3", tag="raw", bufs=3, align_bytes=64)
                nc.sync.dma_start(
                    out=raw[:],
                    in_=w3[a * KP : (a + 1) * KP, b * KP : (b + 1) * KP].rearrange("(p j) c -> p j c", j=PACK),
                )
                w3raw[(a, b)] = raw
                if b == 0:
                    w3g[a] = keep.tile([P, 2 * KP * PACK], BF16, name="w3g%d" % a, align_bytes=64)
            qs = slice(half * P // 2, (half + 1) * P // 2)
            nc.scalar.copy(
                w3g[a][:, b * KP * PACK : (b + 1) * KP * PACK].rearrange(
                    "p (t q j) -> p q t j", t=PACK, j=PACK
                )[:, qs, :, :],
                w3raw[(a, b)][:].rearrange("p j (q t) -> p q t j", t=PACK)[:, qs, :, :],
            )

        h1 = {}
        h2 = {}
        base_t = {}
        fw = {}
        zt = {}
        zf = {}
        zf0 = keep.tile([P, JT * KP], F32, name="zf0")
        zb0 = keep.tile([P, EARLY * KP], BF16, name="zb0", align_bytes=64)

        h2_ps = {}

        def make_h2(s, b):
            h2_ps[s] = bank(b, 1, [P, S], "h2_ps")
            nc.tensor.matmul_mx(
                out=h2_ps[s][:], lhsT=w2w[:, 2 * P * s : 2 * P * (s + 1)].bitcast(FP4X4),
                lhsT_scale=w2s[:, P * s : P * (s + 1)], rhs=v2w[:].bitcast(FP8X4), rhs_scale=v2s[:],
                start=True, stop=True,
            )

        def clamp_h2(s):
            if s == LEAD - 1:
                h2[s] = ring.tile([P, S], F32, name="h2_held", tag="hold", bufs=1, align_bytes=64)
            else:
                h2[s] = ring.tile([P, S], F32, name="h2", tag="h", bufs=4)
            nc.vector.tensor_scalar(h2[s][:], h2_ps[s][:], cols[:, s : s + 1], None, ALU.max)

        def make_h1(s, b):
            acc = bank(b, 1, [P, S], "h1_ps")
            for a in range(2):
                nc.tensor.matmul_mx(
                    out=acc[:], lhsT=w1c[:, w1_cols(a, s)].bitcast(FP8X4),
                    lhsT_scale=w1s[:, w1_cols(a, s)], rhs=v1w[a][:].bitcast(FP8X4),
                    rhs_scale=v1s[4 * a : P, :], start=(a == 0), stop=(a == 1),
                )
            if s == SLICES - 1:
                h = ring.tile([P, S], F32, name="h1_last", tag="latest", bufs=1, align_bytes=64)
            else:
                h = ring.tile([P, S], F32, name="h1", tag="h", bufs=4)
            nc.scalar.activation(h[:], acc[:], ACT.Tanh)
            nc.scalar.activation(h[:], h[:], ACT.Copy, scale=cols[:, SLICES + s : SLICES + s + 1])
            h1[s] = h

        def load_base(s):
            t = ring.tile([P, T2], F32, name="base_t", tag="base", bufs=4)
            nc.sync.dma_start(out=t[:], in_=base[s * P : (s + 1) * P, :])
            base_t[s] = t

        def add_turned(s, src, first, last):
            for half in range(2):
                if first:
                    fw[(s, half)] = bank(2 + 2 * (s % 2) + half, 1, [P, 4, P], "fw")
                for g in range(4):
                    jt = 4 * half + g
                    nc.tensor.matmul(
                        fw[(s, half)][:, g, :], src[:, jt * P : (jt + 1) * P], ident[:],
                        start=(first and g == 0), stop=(last and g == 3), is_transpose=True,
                    )
                if last:
                    a, quarter = divmod(s, 4)
                    if quarter == 0:
                        zt[(a, half)] = ring.tile([P, 4, PACK, P], F32, name="zt", tag="zt", bufs=4)
                    nc.scalar.copy(
                        zt[(a, half)][:, :, :, 32 * quarter : 32 * (quarter + 1)],
                        fw[(s, half)][:].rearrange("j g (q t) -> j g t q", t=PACK),
                    )

        def turn_back(a, pair, zb, first_bank):
            banks = bank(first_bank, 2, [P, 2, PACK, P], "bk")
            if a == 0:
                zf[(a, pair)] = zf0[:, 2 * pair * KP : 2 * (pair + 1) * KP].rearrange("p (u c) -> p u c", u=2)
            else:
                zf[(a, pair)] = ring.tile([P, 2, KP], F32, name="zf1", tag="base", bufs=4)
            for u in range(2):
                jt = 2 * pair + u
                for t in range(PACK):
                    nc.tensor.transpose(banks[:, u, t, :], zt[(a, jt // 4)][:, jt % 4, t, :], ident[:])
            for u in range(2):
                jt = 2 * pair + u
                woven = banks[:, u, :, :].rearrange("p t j -> p j t")
                if a == 1 or jt < EARLY:
                    nc.scalar.copy(zb[:, jt * KP : (jt + 1) * KP].rearrange("p (j t) -> p j t", t=PACK), woven)
                nc.scalar.copy(zf[(a, pair)][:, u, :].rearrange("p (j t) -> p j t", t=PACK), woven)

        def scatter(page, idx, h, wg):
            nc.vector.tensor_tensor(page[:].indirect(idx[:]), h[:], wg[:], ALU.mult)

        steps = [("b", s) for s in range(LEAD)]
        steps.extend([("a", s) for s in range(LEAD)])
        for s in range(LEAD, SLICES):
            steps.extend([("b", s), ("a", s)])

        def make_h(k):
            kind, s = steps[k]
            if kind == "a":
                make_h1(s, k % 2)
            else:
                make_h2(s, k % 2)

        def operand(width, name, pool_tag):
            if pool_tag:
                codes = ring.tile([P, width], U32, name=name + "c", tag=pool_tag[0], bufs=pool_tag[1], align_bytes=64)
            else:
                codes = keep.tile([P, width], U32, name=name + "c", align_bytes=64)
            scales = keep.tile([P, width], U8, name=name + "s", align_bytes=64)
            return codes, scales

        def quantise(dst, c0, src):
            w = src.shape[1] // PACK
            nc.vector.quantize_mx(out=dst[0][:, c0 : c0 + w].bitcast(FP8X4), scales=dst[1][:, c0 : c0 + w], in_=src)

        z0q = [operand(EARLY * P, "z0q0", None)]

        page_of = {"a": pa, "b": pb}
        placed = set()
        added = set()

        def add_ready():
            for s in range(SLICES):
                if s >= 2 and ("a", s - 2) not in added:
                    continue
                if ("base", s) not in added and s in base_t:
                    add_turned(s, base_t[s], True, False)
                    added.add(("base", s))
                for kind in ("b", "a"):
                    if ("base", s) in added and (kind, s) in placed and (kind, s) not in added:
                        add_turned(s, page_of[kind][s % PAGES], False, kind == "a")
                        added.add((kind, s))

        base_at = {1: [0, 1], 2: [2], 3: [3], 4: [4], 6: [5], 8: [6], 10: [7]}
        w1_at = {2: [(1, 0)], 3: [(1, 1)], 4: [(2, 0)], 5: [(2, 1)]}
        w3_at = {6: [(0, 0, 0), (0, 0, 1)], 7: [(0, 1, 0)], 9: [(0, 1, 1)], 10: [(1, 0, 0)], 11: [(1, 0, 1)],
                 13: [(1, 1, 0)], 14: [(1, 1, 1)]}
        back_at = {8: 0, 9: 1, 11: 2, 12: 3}

        make_h(0)
        clamp_h2(0)
        make_h(1)
        w1_cast(0, 0)
        w1_cast(0, 1)
        idx3 = load_list(offs3, "idx3")
        wg1t = ring.tile([P, S], F32, name="wg1t", tag="late", bufs=1, align_bytes=64)
        nc.sync.dma_start(out=wg1t[:], in_=wg1)
        for k in range(len(steps)):
            kind, s = steps[k]
            if k == 1:
                v1w.append(gather(t1w[1][:].bitcast(U32), U32, idx1, "v1w1"))
                v1s = gather(t1s[:], U8, idx1, "v1s")
            if k + 2 < len(steps):
                make_h(k + 2)
            add_ready()
            for c, a in w1_at.get(k, []):
                w1_cast(c, a)
            for sb in base_at.get(k, []):
                load_base(sb)
            for a, b, half in w3_at.get(k, []):
                w3_cast(a, b, half)
            if k == 8:
                load_plane(w4s, w4_scales)
                w4w = [load_words(w4_words[a], "w4w%d" % a) for a in range(2)]
            if k in back_at:
                turn_back(0, back_at[k], zb0, 6)
            if k == 10:
                quantise(z0q[0], 0, zb0[:, 0 : EARLY * KP])
            if k == len(steps) - 1:
                w3q = [operand(H, "w3q0", ("later", 1))]
                quantise(w3q[0], 0, w3g[0][:])
            if k + 1 < len(steps) and steps[k + 1][0] == "b":
                clamp_h2(steps[k + 1][1])
            if kind == "a":
                scatter(pa[s % PAGES], idx3, h1[s], wg1t)
            else:
                scatter(pb[s % PAGES], idx4, h2[s], wg2t)
            placed.add((kind, s))

        late = operand(H + T2 - EARLY * P, "late", ("late", 1))
        w3q.append((late[0][:, 0:H], late[1][:, 0:H]))
        z0q.append((late[0][:, H:], late[1][:, H:]))
        zb1 = ring.tile([P, JT * KP], BF16, name="zb1", tag="raw", bufs=3, align_bytes=64)
        z1q = operand(T2, "z1q", ("raw", 3))

        acc3 = {}
        acc_bank = [0, 1, 2, 3, 0, 1, 2, 3, 0, 1, 2, 3, 4, 5, 0, 1]

        def product_pass(jt, b, a):
            if a == 0:
                acc3[(jt, b)] = bank(acc_bank[2 * jt + b], 1, [P, PACK, P], "acc3")
                z, c0 = (z0q[0], jt * P) if jt < EARLY else (z0q[1], (jt - EARLY) * P)
            else:
                z, c0 = z1q, jt * P
            for t in range(PACK):
                cs = slice(b * KP + t * P, b * KP + (t + 1) * P)
                nc.tensor.matmul_mx(
                    out=acc3[(jt, b)][:, t, :], lhsT=w3q[a][0][:, cs].bitcast(FP8X4), lhsT_scale=w3q[a][1][:, cs],
                    rhs=z[0][:, c0 : c0 + P].bitcast(FP8X4), rhs_scale=z[1][:, c0 : c0 + P],
                    start=(a == 0 and t == 0), stop=(a == 1 and t == PACK - 1),
                )

        groups = [(0, 2), (2, 2), (4, 2), (6, 1), (7, 1)]
        group_of = {}
        for g, (j0, n) in enumerate(groups):
            for u in range(n):
                group_of[j0 + u] = (g, u)
        yb = {}
        yq = {}

        def make_y(jt, b):
            g, u = group_of[jt]
            if b == 0 and u == 0:
                yb[g] = ring.tile([P, 2 * groups[g][1] * KP], BF16, name="yb", tag="yb", bufs=2, align_bytes=64)
            c0 = (b * groups[g][1] + u) * KP
            nc.vector.tensor_tensor(
                yb[g][:, c0 : c0 + KP].rearrange("p (j t) -> p j t", t=PACK),
                acc3[(jt, b)][:].rearrange("p t j -> p j t"),
                zf[(b, jt // 2)][:, jt % 2, :].rearrange("p (j t) -> p j t", t=PACK),
                ALU.max,
            )

        def quant_y(g):
            w = 2 * groups[g][1] * P
            codes = ring.tile([P, w], U32, name="yc", tag="yc", bufs=2, align_bytes=64)
            scales = ring.tile([P, w], U8, name="ys", tag="ys", bufs=2, align_bytes=64)
            yq[g] = (codes, scales)
            quantise(yq[g], 0, yb[g][:])

        def scores(g):
            j0, n_jt = groups[g]
            w = n_jt * P
            codes, scales = yq[g]
            if n_jt == 2:
                acc = bank(6, 2, [P, 4, w], "o_ps")
            else:
                acc = bank(6 + j0 % 2, 1, [P, 4, w], "o_ps")
            for n in range(N // P):
                for b in range(2):
                    nc.tensor.matmul_mx(
                        out=acc[:, n, :], lhsT=w4w[b][:, n * P : (n + 1) * P].bitcast(FP8X4),
                        lhsT_scale=w4s[4 * b : P, n * P : (n + 1) * P],
                        rhs=codes[:, b * w : (b + 1) * w].bitcast(FP8X4), rhs_scale=scales[:, b * w : (b + 1) * w],
                        start=(b == 0), stop=(b == 1),
                    )
            res = ring.tile([P, N // P, w], F32, name="res", tag="res", bufs=3)
            if n_jt == 2:
                nc.scalar.copy(res[:, 0:2, :], acc[:, 0:2, :])
                nc.scalar.copy(res[:, 2, :], acc[:, 2, :])
            else:
                nc.scalar.copy(res[:], acc[:, 0:3, :])
            nc.sync.dma_start(
                out=out[:, j0 * P : j0 * P + w].rearrange("(n p) j -> p n j", p=P), in_=res[:]
            )

        def quant_z1(j0, n):
            quantise(z1q, j0 * P, zb1[:, j0 * KP : (j0 + n) * KP])

        for jt in range(2):
            for b in range(2):
                product_pass(jt, b, 0)
        add_ready()
        zb0_late = ring.tile([P, (JT - EARLY) * KP], BF16, name="zb0_late", tag="latest", bufs=1, align_bytes=64)
        nc.vector.tensor_copy(zb0_late[:], zf0[:, EARLY * KP : JT * KP])
        quantise(w3q[1], 0, w3g[1][:])
        quantise(z0q[1], 0, zb0_late[:, 0 : 2 * KP])
        quantise(z0q[1], 2 * P, zb0_late[:, 2 * KP : 6 * KP])
        turn_back(1, 0, zb1, 6)
        turn_back(1, 1, zb1, 4)
        quant_z1(0, 1)
        for b in range(2):
            product_pass(0, b, 1)
        quant_z1(1, 1)
        for jt in range(JT):
            if jt == 0:
                turn_back(1, 2, zb1, 6)
            if jt == 2:
                turn_back(1, 3, zb1, 4)
            if jt + 1 < JT:
                for b in range(2):
                    product_pass(jt + 1, b, 1)
            make_y(jt, 0)
            if jt + 2 < JT:
                product_pass(jt + 2, 0, 0)
            done = [g for g, (j0, n) in enumerate(groups) if j0 + n == jt]
            for g in done:
                quant_y(g)
            if jt in (0, 2, 4):
                quant_z1(jt + 2, 2)
            make_y(jt, 1)
            if jt + 2 < JT:
                product_pass(jt + 2, 1, 0)
            for g in done:
                scores(g)
        quant_y(len(groups) - 1)
        scores(len(groups) - 1)
